import numpy as np, ml_dtypes
CORES = [3,5,19,21,35,37,51,53,67,69]
N = 10
import mx_ref
BF = ml_dtypes.bfloat16
def entries(a):
    return np.ascontiguousarray(a.T).reshape(-1)
def table(e):
    return np.ascontiguousarray(np.reshape(e, (-1, 16)).T).astype(np.int32)
def cols(t, e):
    v = np.concatenate([t.reshape(128, -1, 4), np.zeros((128, 1, 4), BF)], axis=1)
    return np.ascontiguousarray(v[:, e]).reshape(128, -1)
def f(rng, *shape):
    return mx_ref.flush((rng.standard_normal(shape, dtype=np.float32) * np.exp2(rng.integers(-2, 3, shape[:-1] + (1,)))).astype(BF))
def wide(rng, *shape, cols=0):
    v = rng.standard_normal(shape, dtype=np.float32) * np.exp2(rng.integers(-12, 13, shape)).astype(np.float32)
    if cols: v *= np.repeat(np.exp2(rng.integers(-cols, cols + 1, shape[:-2] + (1, shape[-1] // 4))) * (rng.random(shape[:-2] + (1, shape[-1] // 4)) > 0.0625), 4, axis=-1).astype(np.float32)
    return mx_ref.flush(v.astype(BF))
T, CAPP = 256, 32
def even(n):
    return [T // n + (k < T % n) for k in range(n)]
def counts(rng, h, moves=10 * N * N):
    n = np.array([[h[(d - s) % N] for d in range(N)] for s in range(N)])[rng.permutation(N)][:, rng.permutation(N)]
    top = np.where(n > 0, CAPP, 0)
    for _ in range(moves):
        a, b = rng.permutation(N)[:2]; c, e = rng.permutation(N)[:2]
        k = rng.integers(0, min(n[a, e], n[b, c], top[a, c] - n[a, c], top[b, e] - n[b, e]) + 1)
        n[a, c] += k; n[b, e] += k; n[a, e] -= k; n[b, c] -= k
    return n
def lists(rng, n, back=False):
    a = np.full((N, N, CAPP), -1)
    for s in range(N):
        p = np.arange(T)[::-1] if back else rng.permutation(T)
        for d in range(N):
            k = rng.permutation(CAPP)[:n[s, d]]
            if back: k = np.sort(k)
            a[s, d, k] = p[:n[s, d]]; p = p[n[s, d]:]
    m = []
    for d in range(N):
        k = np.flatnonzero(a[:, d].reshape(-1) >= 0)
        m.append(table(k[::-1] if back else rng.permutation(k)))
    return {"send": np.stack([table(a[s].reshape(-1)) for s in range(N)]), "mine": np.stack(m), "prev": np.stack([m[(r - 1) % N] for r in range(N)])}
def setup_inputs(rng):
    return {"x": f(rng, N, 128, 4 * T), **lists(rng, counts(rng, even(N)))}
def setup_inputs_empty(rng):
    return {**setup_inputs(rng), **lists(rng, counts(rng, even(N - 1) + [0]))}
def setup_inputs_full(rng):
    return {**setup_inputs(rng), **lists(rng, counts(rng, [min(CAPP, max(0, T - k * CAPP)) for k in range(N)], 0))}
def setup_inputs_reversed(rng):
    return {**setup_inputs(rng), **lists(rng, counts(rng, even(N)), back=True)}
def setup_inputs_spread(rng):
    d = setup_inputs(rng); d["x"] = wide(rng, N, 128, 4 * T, cols=8); return d
def check_inputs(d):
    b = []
    v = np.abs(np.asarray(d["x"]).astype(np.float32))
    if not ((v == 0) | ((v >= 2.0 ** -30) & (v <= 2.0 ** 30))).all(): b.append("x")
    for r in range(N):
        c, m = entries(d["send"][r]), entries(d["mine"][r])
        if c.min() < -1 or not np.array_equal(np.sort(c[c >= 0]), np.arange(T)): b.append("send")
        arrived = np.concatenate([entries(d["send"][s])[r * CAPP:(r + 1) * CAPP] for s in range(N)])
        if not np.array_equal(np.sort(m), np.flatnonzero(arrived >= 0)): b.append("mine")
        if not np.array_equal(d["prev"][r], d["mine"][(r - 1) % N]): b.append("prev")
    return b
def reference(x, send, mine, prev):
    K = []
    for r in range(N):
        arrived = np.concatenate([cols(x[s], entries(send[s])[r * CAPP:(r + 1) * CAPP]) for s in range(N)], axis=1)
        K.append(cols(arrived, entries(mine[r])))
    Q = [mx_ref.quantize(t) for t in K]
    y = np.zeros((N, T, 2 * T), np.float32)
    for r in range(N):
        for p in range(T // 128):
            W = mx_ref.quantize(np.ascontiguousarray(K[r][:, 512 * p:512 * p + 512]))
            y[r, 128 * p:128 * p + 128, :T] = mx_ref.matmul(W, Q[r])
            y[r, 128 * p:128 * p + 128, T:] = mx_ref.matmul(W, Q[(r - 1) % N])
    return {"y": y}

@@ -1,0 +1,263 @@
+from concourse.bass import DstId, RemoteDMATransfer, IndirectOffsetOnAxis
+from concourse.mybir import dt, AluOpType, ActivationFunctionType
+
+N = 10
+COLS = 256
+CAP = 32
+RUN = 2 * CAP
+SLOTS = N * CAP
+MOV = N * RUN
+LW = 2 * N
+BW = COLS // 16
+NOROW = 4096
+
+SCRATCH = {
+    "snd": ("sbuf", [128, LW], "int32"),
+    "soff": ("sbuf", [128, LW], "uint16"),
+    "xs": ("sbuf", [128, 4 * COLS], "bfloat16"),
+    "h": ("sbuf", [128, 4 * SLOTS], "bfloat16"),
+    "qc": ("sbuf", [128, SLOTS], "float8_e4m3fn_x4"),
+    "qs": ("sbuf", [128, SLOTS], "uint8"),
+    "mc": ("sbuf", [128, MOV], "float8_e4m3fn_x4"),
+    "ms": ("sbuf", [128, MOV], "uint8"),
+    "wc": ("sbuf", [128, 256], "float8_e4m3fn_x4"),
+    "ws": ("sbuf", [128, 256], "uint8"),
+    "lm": ("sbuf", [128, 2 * BW], "int32"),
+    "k_t": ("sbuf", [128, 2 * BW], "int32"),
+    "k_b": ("sbuf", [128, 2 * BW], "int32"),
+    "k_m": ("sbuf", [128, 2 * BW], "int32"),
+    "k_f": ("sbuf", [128, BW], "int32"),
+    "k_g": ("sbuf", [128, BW], "int32"),
+    "k_d": ("sbuf", [128, 2 * BW], "int32"),
+    "k_e": ("sbuf", [128, 2 * BW], "int32"),
+    "k_p": ("sbuf", [128, BW], "int32"),
+    "coff": ("sbuf", [128, 2 * BW], "uint16"),
+    "woff": ("sbuf", [128, BW], "uint16"),
+    "nul": ("sbuf", [128, COLS], "float32"),
+    "one": ("sbuf", [128, COLS], "float32"),
+    "num": ("sbuf", [128, COLS], "float32"),
+    "inv": ("sbuf", [128, SLOTS], "int32"),
+    "idx": ("sbuf", [128, 4], "int32"),
+    "pp": ("psum", [128, 512 * 8], "float32"),
+}
+SEMAPHORES = ["l_send", "l_x", "l_lm", "l_g", "offa", "offb", "gva", "gsa", "gvb", "gsb", "qa", "qb",
+              "k1", "k2", "k3", "k4", "k5", "k6", "k7", "cst", "fil", "numd", "invd", "selfc", "rp", "r1", "r2", "r3", "r4",
+              "ca", "cb", "idxd", "sent", "stored"]
+for _t in "dab":
+    SCRATCH["s_" + _t] = ("sbuf", [128, MOV], "float32")
+    SCRATCH["o_" + _t] = ("sbuf", [128, 2 * COLS], "float32")
+    SEMAPHORES += [_n + _t + str(_p) for _n in ("mm", "cp") for _p in range(4 if _t == "d" else 2)] + ["ov" + _t, "os" + _t]
+
+
+def place(s, r):
+    return (s - (r - r % 2)) % N
+
+
+def slot_pos(s, d):
+    return (s - 1 - d) % N if s % 2 else (d - s) % N
+
+
+def rank_program(g, core, T, topo):
+    r = T.rank_of(core)
+    if r is None:
+        return
+    V, S, P, Y, sem = g.vector, g.scalar, g.tensor, g.sync, T.sem
+    OP, COPY = AluOpType, ActivationFunctionType.Copy
+    rising = r % 2 == 0
+
+    for q in range(8):
+        e = S if q < 4 else Y
+        e.dma_start(T.snd[16 * q:16 * q + 16, :], T.send[:]).then_inc(sem.l_send, 16)
+    Y.dma_start(T.xs[:], T.x[:]).then_inc(sem.l_x, 16)
+    g.dma_start(T.lm[0:16, 0:BW], T.mine[:]).then_inc(sem.l_g, 16)
+    for q in range(8):
+        if q:
+            Y.dma_start(T.lm[16 * q:16 * q + 16, 0:BW], T.mine[:]).then_inc(sem.l_lm, 16)
+        Y.dma_start(T.lm[16 * q:16 * q + 16, BW:2 * BW], T.prev[:]).then_inc(sem.l_lm, 16)
+
+    V.memset(T.nul[:], 0.0).then_inc(sem.cst, 1)
+    V.memset(T.one[:], 1.0).then_inc(sem.cst, 1)
+    V.memset(T.inv[:], NOROW).then_inc(sem.fil, 1)
+    V.wait_ge(sem.cst, 2)
+    V.tensor_tensor_scan(T.num[:], T.nul[:], T.one[:], -1.0, OP.add, OP.add).then_inc(sem.numd, 1)
+    V.wait_ge(sem.l_send, 128)
+    stage = [(0, 4), (4, 10)] if rising else [(6, 10), (0, 6)]
+
+    def offsets(lo, hi, done):
+        n, k = 0, lo
+        while k < hi:
+            slot = (r + k) % N if rising else (r - 1 - k) % N
+            m = min(hi - k, N - slot if rising else slot + 1)
+            if rising:
+                V.tensor_scalar(T.soff[:, 2 * k:2 * (k + m)], T.snd[:, 2 * slot:2 * (slot + m)], 4, 0, OP.mult, OP.max).then_inc(done, 1)
+                n += 1
+            else:
+                for b in range(2):
+                    first, stop = 2 * slot + b, 2 * (slot - m + 1) + b - 1
+                    src = T.snd[:, first::-2] if stop < 0 else T.snd[:, first:stop:-2]
+                    V.tensor_scalar(T.soff[:, 2 * k + b:2 * (k + m):2], src, 4, 0, OP.mult, OP.max).then_inc(done, 1)
+                    n += 1
+            k += m
+        return n
+
+    n_off = [offsets(*stage[0], sem.offa), offsets(*stage[1], sem.offb)]
+    off_s, gv, gs, qd = [sem.offa, sem.offb], [sem.gva, sem.gvb], [sem.gsa, sem.gsb], [sem.qa, sem.qb]
+
+    for w in range(2):
+        lo, hi = stage[w]
+        for t in range(4):
+            e = V if t < 2 else S
+            if t % 2 == 0:
+                e.wait_ge(off_s[w], n_off[w])
+                if w == 0:
+                    e.wait_ge(sem.l_x, 16)
+            out = T.h[:, 128 * lo + t:128 * hi:4]
+            src = T.xs[:, t:4 * COLS].indirect(T.soff[:, 2 * lo:2 * hi])
+            if t < 2:
+                V.tensor_copy(out, src).then_inc(gv[w], 1)
+            else:
+                S.activation(out, src, COPY).then_inc(gs[w], 1)
+        V.wait_ge(gv[w], 2)
+        V.wait_ge(gs[w], 2)
+        V.quantize_mx(T.qc[:, CAP * lo:CAP * hi], T.qs[:, CAP * lo:CAP * hi], T.h[:, 128 * lo:128 * hi]).then_inc(qd[w], 1)
+
+    others = [(r + k) % N for k in range(1, N)]
+    far = [d for d in others if topo.chip(T.cores[d]) != topo.chip(core)]
+    near = [d for d in others if d not in far]
+    arrive = {8: sem.r1, 6: sem.r2, 4: sem.r3, 2: sem.r4, 0: sem.rp}
+    n_sent = 0
+    for w in range(4):
+        pair = far[2 * w:2 * w + 2]
+        eng = {}
+        for i, d in enumerate(pair):
+            e = topo.engines(core, T.cores[d])
+            eng[d] = e[len(e) // 2 * i:len(e) // 2 * (i + 1)]
+        if w == 1:
+            used = topo.engines(core, T.cores[far[0]])
+            for d in near:
+                eng[d] = [e for e in topo.engines(core, T.cores[d]) if e not in used][:2]
+        if w < 2:
+            g.wait_ge(qd[w], 1)
+        for part in range(2):
+            moves = []
+            for d in eng:
+                a = CAP * min(slot_pos(r, d), slot_pos(r, (d - 1) % N))
+                v = place(r, d)
+                rid, pid, _ = topo.addr(T.cores[d])
+                if part == 0:
+                    src, dst = T.qc[:, a:a + RUN].bitcast(dt.uint8), T.mc[:, RUN * v:RUN * v + RUN].bitcast(dt.uint8)
+                else:
+                    src, dst = T.qs[:, a:a + RUN], T.ms[:, RUN * v:RUN * v + RUN]
+                moves.append(RemoteDMATransfer(
+                    dst_ids=[DstId(rid=rid, pnc=pid)], dma_engine_mask=sum(1 << e for e in eng[d]),
+                    remote_sem=arrive[v - v % 2], src=src, dst=dst))
+                n_sent += len(eng[d])
+            g.remote_dma_fused(moves, local_sem=sem.sent)
+    n_wave, n_near = 16, 4
+
+    def copy(dc, ds, a, sc, ss, b, n, done):
+        Y.dma_start(dc[:, a:a + n].bitcast(dt.uint8), sc[:, b:b + n].bitcast(dt.uint8)).then_inc(done, 16)
+        Y.dma_start(ds[:, a:a + n], ss[:, b:b + n]).then_inc(done, 16)
+
+    def draw(a, pos, done):
+        copy(T.wc, T.ws, a, T.mc, T.ms, RUN * pos + CAP, 64, done)
+
+    Y.wait_ge(sem.qa, 1)
+    Y.wait_ge(sem.qb, 1)
+    v = place(r, r)
+    own, prv = CAP * slot_pos(r, r), CAP * slot_pos(r, (r - 1) % N)
+    copy(T.mc, T.ms, RUN * v + (CAP if rising else 0), T.qc, T.qs, own, CAP, sem.selfc)
+    copy(T.mc, T.ms, RUN * v + (0 if rising else CAP), T.qc, T.qs, prv, CAP, sem.selfc)
+    Y.wait_ge(sem.r2, n_wave)
+    draw(64, 6, sem.ca)
+    Y.wait_ge(sem.selfc, 64)
+    Y.wait_ge(sem.rp, n_near)
+    draw(0, 0, sem.ca)
+    Y.wait_ge(sem.r3, n_wave)
+    draw(192, 4, sem.cb)
+    Y.wait_ge(sem.r4, n_wave)
+    draw(128, 2, sem.cb)
+
+    base = r - r % 2
+    mn, pv = slice(0, BW), slice(BW, 2 * BW)
+    V.wait_ge(sem.l_lm, 15 * 16)
+    V.wait_ge(sem.l_g, 16)
+    V.tensor_scalar(T.k_t[:], T.lm[:], CAP * base, SLOTS, OP.is_lt, OP.mult).then_inc(sem.k1, 1)
+    V.wait_ge(sem.k1, 1)
+    V.tensor_tensor(T.k_b[:], T.lm[:], T.k_t[:], OP.add).then_inc(sem.k2, 1)
+    V.wait_ge(sem.k2, 1)
+    V.tensor_scalar(T.woff[:], T.k_b[:, mn], -CAP * base, None, OP.add).then_inc(sem.k3, 1)
+    V.wait_ge(sem.k3, 1)
+    V.wait_ge(sem.fil, 1)
+    V.wait_ge(sem.numd, 1)
+    V.tensor_copy(T.inv[:].indirect(T.woff[:]), T.num[:]).then_inc(sem.invd, 1)
+    V.tensor_scalar(T.k_m[:], T.k_b[:], RUN - 1, None, OP.bitwise_and).then_inc(sem.k4, 1)
+    V.tensor_scalar(T.k_f[:], T.k_b[:, pv], CAP, None, OP.bitwise_and).then_inc(sem.k4, 1)
+    V.tensor_scalar(T.k_d[:], T.k_b[:], 2, -RUN * base, OP.mult, OP.add).then_inc(sem.k4, 1)
+    V.wait_ge(sem.k4, 3)
+    V.tensor_tensor(T.k_e[:], T.k_d[:], T.k_m[:], OP.subtract).then_inc(sem.k5, 1)
+    V.tensor_scalar(T.k_g[:], T.k_f[:], 2, None, OP.mult).then_inc(sem.k5, 1)
+    V.wait_ge(sem.k5, 2)
+    V.tensor_tensor(T.k_p[:], T.k_e[:, pv], T.k_g[:], OP.add).then_inc(sem.k6, 1)
+    V.tensor_scalar(T.coff[:, mn], T.k_e[:, mn], CAP, None, OP.add).then_inc(sem.k7, 1)
+    V.wait_ge(sem.k6, 1)
+    V.tensor_copy(T.coff[:, pv], T.k_p[:]).then_inc(sem.k7, 1)
+
+    S.wait_ge(sem.invd, 1)
+    for col, p, a, n in ((0, 0, 256, 64), (1, 0, 0, 64), (1, 64, 192, 64), (2, 0, 64, 128)):
+        S.dma_start(T.idx[p:p + n, col:col + 1], T.inv[0:1, a:a + n]).then_inc(sem.idxd, 16)
+
+    tiles = {
+        "d": (T.mc, T.ms, 8 * RUN, [(6 * RUN, 10 * RUN, 0, S), (0, 2 * RUN, 1, V), (4 * RUN, 6 * RUN, 2, S), (2 * RUN, 4 * RUN, 3, V)]),
+        "a": (T.wc, T.ws, 0, [(0, 5 * RUN, 4, V), (5 * RUN, 10 * RUN, 5, S)]),
+        "b": (T.wc, T.ws, 128, [(0, 5 * RUN, 6, V), (5 * RUN, 10 * RUN, 7, S)]),
+    }
+
+    def product(tile, i):
+        c, s, a, parts = tiles[tile]
+        lo, hi, bank, _ = parts[i]
+        P.matmul_mx(T.pp[:, 512 * bank:512 * bank + hi - lo], c[:, a:a + 128], s[:, a:a + 128],
+                    T.mc[:, lo:hi], T.ms[:, lo:hi], True, True).then_inc(sem["mm%s%d" % (tile, i)], 1)
+
+    P.wait_ge(sem.r1, n_wave)
+    P.wait_ge(sem.r2, n_wave)
+    product("d", 0)
+    P.wait_ge(sem.selfc, 64)
+    P.wait_ge(sem.rp, n_near)
+    product("d", 1)
+    P.wait_ge(sem.r3, n_wave)
+    product("d", 2)
+    P.wait_ge(sem.r4, n_wave)
+    product("d", 3)
+    for tile, done in (("a", sem.ca), ("b", sem.cb)):
+        P.wait_ge(done, 64)
+        product(tile, 0)
+        product(tile, 1)
+
+    V.wait_ge(sem.k7, 2)
+    S.wait_ge(sem.k7, 2)
+    for tile in "dab":
+        parts = tiles[tile][3]
+        buf, out = T["s_" + tile], T["o_" + tile]
+        for i, (lo, hi, bank, e) in enumerate(parts):
+            e.wait_ge(sem["mm%s%d" % (tile, i)], 1)
+            src = T.pp[:, 512 * bank:512 * bank + hi - lo]
+            done = sem["cp%s%d" % (tile, i)]
+            if e is V:
+                V.tensor_copy(buf[:, lo:hi], src).then_inc(done, 1)
+            else:
+                S.activation(buf[:, lo:hi], src, COPY).then_inc(done, 1)
+        for i in range(len(parts)):
+            V.wait_ge(sem["cp%s%d" % (tile, i)], 1)
+            S.wait_ge(sem["cp%s%d" % (tile, i)], 1)
+        V.tensor_copy(out[:, 0:COLS], buf[:].indirect(T.coff[:, mn])).then_inc(sem["ov" + tile], 1)
+        S.activation(out[:, COLS:2 * COLS], buf[:].indirect(T.coff[:, pv]), COPY).then_inc(sem["os" + tile], 1)
+
+    g.wait_ge(sem.idxd, 64)
+    for col, (tile, lo, n) in enumerate((("d", CAP, 64), ("a", 0, 128), ("b", 0, 128))):
+        g.wait_ge(sem["ov" + tile], 1)
+        g.wait_ge(sem["os" + tile], 1)
+        g.indirect_dma_start(T.y[:], IndirectOffsetOnAxis(ap=T.idx[0:n, col:col + 1], axis=0),
+                             T["o_" + tile][lo:lo + n, :], None, bounds_check=COLS - 1, oob_is_err=False).then_inc(sem.stored, 16)
+    g.wait_ge(sem.sent, n_sent)
+    g.wait_ge(sem.stored, 48)

@@ -9,52 +9,56 @@ SLOTS = N * CAP
 MOV = N * RUN
 LW = 2 * N
 BW = COLS // 16
-NOROW = 4096
+NOROW = 4096.0
+
+
+def blocks(text):
+    return [(int(w[0]), w[1]) for w in text.split()]
+
+
+SENT = [(k, "q") for k in range(N - 1)]
+LAYOUT = [
+    SENT + blocks("0p 1p 8p 8o 8j 7j 7o 7p 4p 4o 0o 1o 5o 5p 2p 2o 9o 9p 6p 6o 3o 3p"),
+    blocks("2p 2o 3o 3p 8p 8o 7o 7p 4p 4o 1o 0o 9o 9p 9j 6j 6p 6o 5o 5p 0p 1p") + SENT,
+]
+WIDTH = CAP * len(LAYOUT[0])
+TILE_A = [(4, "o"), (4, "o")]
+TILE_D = [(6, "p"), (8, "p")]
+DRAWN = [[blocks("8o"), blocks("7o"), blocks("2o 9o")], [blocks("6o 5o"), blocks("2o 3o")]]
+EARLY = [[blocks("0p 8o"), blocks("7o 5p")], [blocks("4p 9p"), blocks("6p 1p")]]
+LATE = [[blocks("2p 9p"), blocks("6p 3p")], [blocks("2p 3p"), blocks("8p 7p")]]
+WHOLE = [[blocks("5o 3p"), blocks("0p 8o"), blocks("7o 1o")], [blocks("2p 4o"), blocks("1o 9p"), blocks("6p 1p")]]
+HANDED = [(blocks("8o 7o"), (8, "p")), (blocks("9p 6p"), (9, "o"))]
 
 SCRATCH = {
     "snd": ("sbuf", [128, LW], "int32"),
     "soff": ("sbuf", [128, LW], "uint16"),
     "xs": ("sbuf", [128, 4 * COLS], "bfloat16"),
     "h": ("sbuf", [128, 4 * SLOTS], "bfloat16"),
-    "qc": ("sbuf", [128, SLOTS], "float8_e4m3fn_x4"),
-    "qs": ("sbuf", [128, SLOTS], "uint8"),
-    "mc": ("sbuf", [128, MOV], "float8_e4m3fn_x4"),
-    "ms": ("sbuf", [128, MOV], "uint8"),
-    "wc": ("sbuf", [128, 256], "float8_e4m3fn_x4"),
-    "ws": ("sbuf", [128, 256], "uint8"),
+    "mc": ("sbuf", [128, WIDTH], "float8_e4m3fn_x4"),
+    "ms": ("sbuf", [128, WIDTH], "uint8"),
+    "wc": ("sbuf", [128, 128], "float8_e4m3fn_x4"),
+    "ws": ("sbuf", [128, 128], "uint8"),
     "lm": ("sbuf", [128, 2 * BW], "int32"),
-    "k_t": ("sbuf", [128, 2 * BW], "int32"),
+    "k_a": ("sbuf", [128, 2 * BW], "int32"),
     "k_b": ("sbuf", [128, 2 * BW], "int32"),
-    "k_m": ("sbuf", [128, 2 * BW], "int32"),
-    "k_f": ("sbuf", [128, BW], "int32"),
-    "k_g": ("sbuf", [128, BW], "int32"),
-    "k_d": ("sbuf", [128, 2 * BW], "int32"),
-    "k_e": ("sbuf", [128, 2 * BW], "int32"),
-    "k_p": ("sbuf", [128, BW], "int32"),
-    "coff": ("sbuf", [128, 2 * BW], "uint16"),
-    "woff": ("sbuf", [128, BW], "uint16"),
+    "k_c": ("sbuf", [128, 2 * BW], "int32"),
+    "off": ("sbuf", [128, 3 * BW], "uint16"),
     "nul": ("sbuf", [128, COLS], "float32"),
     "one": ("sbuf", [128, COLS], "float32"),
     "num": ("sbuf", [128, COLS], "float32"),
-    "inv": ("sbuf", [128, SLOTS], "int32"),
+    "inv": ("sbuf", [128, SLOTS], "float32"),
+    "turned": ("sbuf", [128, 3 * CAP], "float32"),
     "idx": ("sbuf", [128, 4], "int32"),
     "pp": ("psum", [128, 512 * 8], "float32"),
 }
-SEMAPHORES = ["l_send", "l_x", "l_lm", "l_g", "offa", "offb", "gva", "gsa", "gvb", "gsb", "qa", "qb",
-              "k1", "k2", "k3", "k4", "k5", "k6", "k7", "cst", "fil", "numd", "invd", "selfc", "rp", "r1", "r2", "r3", "r4",
-              "ca", "cb", "idxd", "sent", "stored"]
-for _t in "dab":
+SEMAPHORES = ["l_send", "l_x", "l_lm", "l_g", "off0", "off1", "gva", "gsa", "gvb", "gsb", "qa", "qb",
+              "k1", "k2", "k3", "k4", "k5", "cst", "fil", "numd", "invd", "selfc", "wide", "early", "late",
+              "drawn", "t_ab", "t_d", "i_ab", "i_d", "c_early", "sent", "stored"]
+for _t in "abd":
     SCRATCH["s_" + _t] = ("sbuf", [128, MOV], "float32")
     SCRATCH["o_" + _t] = ("sbuf", [128, 2 * COLS], "float32")
-    SEMAPHORES += [_n + _t + str(_p) for _n in ("mm", "cp") for _p in range(4 if _t == "d" else 2)] + ["ov" + _t, "os" + _t]
-
-
-def place(s, r):
-    return (s - (r - r % 2)) % N
-
-
-def slot_pos(s, d):
-    return (s - 1 - d) % N if s % 2 else (d - s) % N
+    SEMAPHORES += ["mm" + _t + str(_p) for _p in range(4 if _t == "a" else 3)] + ["c_" + _t, "ov" + _t, "os" + _t]
 
 
 def rank_program(g, core, T, topo):
@@ -63,54 +67,63 @@ def rank_program(g, core, T, topo):
         return
     V, S, P, Y, sem = g.vector, g.scalar, g.tensor, g.sync, T.sem
     OP, COPY = AluOpType, ActivationFunctionType.Copy
-    rising = r % 2 == 0
 
-    for q in range(8):
-        e = S if q < 4 else Y
-        e.dma_start(T.snd[16 * q:16 * q + 16, :], T.send[:]).then_inc(sem.l_send, 16)
+    def first_of(d):
+        return min(k for k in range(N) if topo.chip(T.cores[k]) == topo.chip(T.cores[d]))
+
+    def at(d, block):
+        return CAP * LAYOUT[d - first_of(d)].index(block)
+
+    base = first_of(r)
+    second = r - base
+    near = base + 1 - second
+    lay = LAYOUT[second]
+    q0 = at(r, (1, "p")) if second else 0
+
+    def slot_pos(d):
+        return (r - 1 - d) % N if second else (d - r) % N
+
+    Y.dma_start(T.snd[0:16, :], T.send[:]).then_inc(sem.l_send, 16)
+    S.dma_start(T.snd[16:32, :], T.send[:]).then_inc(sem.l_send, 16)
     Y.dma_start(T.xs[:], T.x[:]).then_inc(sem.l_x, 16)
     g.dma_start(T.lm[0:16, 0:BW], T.mine[:]).then_inc(sem.l_g, 16)
-    for q in range(8):
-        if q:
-            Y.dma_start(T.lm[16 * q:16 * q + 16, 0:BW], T.mine[:]).then_inc(sem.l_lm, 16)
-        Y.dma_start(T.lm[16 * q:16 * q + 16, BW:2 * BW], T.prev[:]).then_inc(sem.l_lm, 16)
+    S.dma_start(T.lm[16:32, 0:BW], T.mine[:]).then_inc(sem.l_lm, 16)
+    S.dma_start(T.lm[0:16, BW:2 * BW], T.prev[:]).then_inc(sem.l_lm, 16)
+    S.dma_start(T.lm[16:32, BW:2 * BW], T.prev[:]).then_inc(sem.l_lm, 16)
 
     V.memset(T.nul[:], 0.0).then_inc(sem.cst, 1)
     V.memset(T.one[:], 1.0).then_inc(sem.cst, 1)
     V.memset(T.inv[:], NOROW).then_inc(sem.fil, 1)
     V.wait_ge(sem.cst, 2)
     V.tensor_tensor_scan(T.num[:], T.nul[:], T.one[:], -1.0, OP.add, OP.add).then_inc(sem.numd, 1)
-    V.wait_ge(sem.l_send, 128)
-    stage = [(0, 4), (4, 10)] if rising else [(6, 10), (0, 6)]
-
-    def offsets(lo, hi, done):
-        n, k = 0, lo
-        while k < hi:
-            slot = (r + k) % N if rising else (r - 1 - k) % N
-            m = min(hi - k, N - slot if rising else slot + 1)
-            if rising:
-                V.tensor_scalar(T.soff[:, 2 * k:2 * (k + m)], T.snd[:, 2 * slot:2 * (slot + m)], 4, 0, OP.mult, OP.max).then_inc(done, 1)
+    V.wait_ge(sem.l_send, 32)
+    n, k = 0, 0
+    while k < N:
+        slot = (r - 1 - k) % N if second else (r + k) % N
+        m = min(N - k, slot + 1 if second else N - slot)
+        if second:
+            for b in range(2):
+                first, stop = 2 * slot + b, 2 * (slot - m + 1) + b - 1
+                src = T.snd[0:32, first::-2] if stop < 0 else T.snd[0:32, first:stop:-2]
+                V.tensor_scalar(T.soff[0:32, 2 * k + b:2 * (k + m):2], src, 4, 0, OP.mult, OP.max).then_inc(sem.off0, 1)
                 n += 1
-            else:
-                for b in range(2):
-                    first, stop = 2 * slot + b, 2 * (slot - m + 1) + b - 1
-                    src = T.snd[:, first::-2] if stop < 0 else T.snd[:, first:stop:-2]
-                    V.tensor_scalar(T.soff[:, 2 * k + b:2 * (k + m):2], src, 4, 0, OP.mult, OP.max).then_inc(done, 1)
-                    n += 1
-            k += m
-        return n
+        else:
+            V.tensor_scalar(T.soff[0:32, 2 * k:2 * (k + m)], T.snd[0:32, 2 * slot:2 * (slot + m)], 4, 0, OP.mult, OP.max).then_inc(sem.off0, 1)
+            n += 1
+        k += m
+    V.wait_ge(sem.off0, n)
+    for a in range(1, 4):
+        V.tensor_copy(T.soff[32 * a:32 * a + 32, :], T.soff[0:32, :]).then_inc(sem.off1, 1)
 
-    n_off = [offsets(*stage[0], sem.offa), offsets(*stage[1], sem.offb)]
-    off_s, gv, gs, qd = [sem.offa, sem.offb], [sem.gva, sem.gvb], [sem.gsa, sem.gsb], [sem.qa, sem.qb]
-
+    stage = [(6, 10), (0, 6)] if second else [(0, 4), (4, 10)]
+    gv, gs, qd = [sem.gva, sem.gvb], [sem.gsa, sem.gsb], [sem.qa, sem.qb]
+    for e in (V, S):
+        e.wait_ge(sem.off0, n)
+        e.wait_ge(sem.off1, 3)
+        e.wait_ge(sem.l_x, 16)
     for w in range(2):
         lo, hi = stage[w]
         for t in range(4):
-            e = V if t < 2 else S
-            if t % 2 == 0:
-                e.wait_ge(off_s[w], n_off[w])
-                if w == 0:
-                    e.wait_ge(sem.l_x, 16)
             out = T.h[:, 128 * lo + t:128 * hi:4]
             src = T.xs[:, t:4 * COLS].indirect(T.soff[:, 2 * lo:2 * hi])
             if t < 2:
@@ -119,145 +132,176 @@ def rank_program(g, core, T, topo):
                 S.activation(out, src, COPY).then_inc(gs[w], 1)
         V.wait_ge(gv[w], 2)
         V.wait_ge(gs[w], 2)
-        V.quantize_mx(T.qc[:, CAP * lo:CAP * hi], T.qs[:, CAP * lo:CAP * hi], T.h[:, 128 * lo:128 * hi]).then_inc(qd[w], 1)
+        a, b = q0 + CAP * lo, q0 + CAP * hi
+        V.quantize_mx(T.mc[:, a:b], T.ms[:, a:b], T.h[:, 128 * lo:128 * hi]).then_inc(qd[w], 1)
 
-    others = [(r + k) % N for k in range(1, N)]
-    far = [d for d in others if topo.chip(T.cores[d]) != topo.chip(core)]
-    near = [d for d in others if d not in far]
-    arrive = {8: sem.r1, 6: sem.r2, 4: sem.r3, 2: sem.r4, 0: sem.rp}
-    n_sent = 0
-    for w in range(4):
-        pair = far[2 * w:2 * w + 2]
-        eng = {}
-        for i, d in enumerate(pair):
-            e = topo.engines(core, T.cores[d])
-            eng[d] = e[len(e) // 2 * i:len(e) // 2 * (i + 1)]
-        if w == 1:
-            used = topo.engines(core, T.cores[far[0]])
-            for d in near:
-                eng[d] = [e for e in topo.engines(core, T.cores[d]) if e not in used][:2]
-        if w < 2:
-            g.wait_ge(qd[w], 1)
-        for part in range(2):
-            moves = []
-            for d in eng:
-                a = CAP * min(slot_pos(r, d), slot_pos(r, (d - 1) % N))
-                v = place(r, d)
+    n_sent = [0]
+
+    def send(moves):
+        for codes, buf in ((True, T.mc), (False, T.ms)):
+            calls = []
+            for d, a, b, m, eng, done in moves:
                 rid, pid, _ = topo.addr(T.cores[d])
-                if part == 0:
-                    src, dst = T.qc[:, a:a + RUN].bitcast(dt.uint8), T.mc[:, RUN * v:RUN * v + RUN].bitcast(dt.uint8)
-                else:
-                    src, dst = T.qs[:, a:a + RUN], T.ms[:, RUN * v:RUN * v + RUN]
-                moves.append(RemoteDMATransfer(
-                    dst_ids=[DstId(rid=rid, pnc=pid)], dma_engine_mask=sum(1 << e for e in eng[d]),
-                    remote_sem=arrive[v - v % 2], src=src, dst=dst))
-                n_sent += len(eng[d])
-            g.remote_dma_fused(moves, local_sem=sem.sent)
-    n_wave, n_near = 16, 4
+                src, dst = buf[:, a:a + m], buf[:, b:b + m]
+                if codes:
+                    src, dst = src.bitcast(dt.uint8), dst.bitcast(dt.uint8)
+                calls.append(RemoteDMATransfer(dst_ids=[DstId(rid=rid, pnc=pid)], dma_engine_mask=sum(1 << e for e in eng),
+                                               remote_sem=done, src=src, dst=dst))
+                n_sent[0] += len(eng)
+            g.remote_dma_fused(calls, local_sem=sem.sent)
 
-    def copy(dc, ds, a, sc, ss, b, n, done):
-        Y.dma_start(dc[:, a:a + n].bitcast(dt.uint8), sc[:, b:b + n].bitcast(dt.uint8)).then_inc(done, 16)
-        Y.dma_start(ds[:, a:a + n], ss[:, b:b + n]).then_inc(done, 16)
+    def halves(e):
+        return e[:len(e) // 2], e[len(e) // 2:]
 
-    def draw(a, pos, done):
-        copy(T.wc, T.ws, a, T.mc, T.ms, RUN * pos + CAP, 64, done)
+    def kept(d, kinds):
+        return min(at(d, ((r - first_of(d)) % N, k)) for k in kinds)
+
+    def slots(*ranks):
+        return q0 + CAP * min(slot_pos(d % N) for d in ranks)
+
+    chips = [(base + 2 * k) % N for k in range(1, N // 2)]
+    off_chip = topo.engines(core, T.cores[chips[0]])
+    on_chip = [e for e in topo.engines(core, T.cores[near]) if e not in off_chip]
+    for w in range(2):
+        c = chips[w]
+        d = c + (second if w == 0 else 1 - second)
+        g.wait_ge(qd[w], 1)
+        send([(d, slots(c - 1, c, c + 1), kept(d, "opj"), 3 * CAP, topo.engines(core, T.cores[d]), sem.wide)])
+    def direct(c, done):
+        send([(d, slots(d - 1, d), kept(d, "op"), RUN, halves(topo.engines(core, T.cores[d]))[d - c], done) for d in (c, c + 1)])
+
+    send([(near, slots(near - k), kept(near, kind), CAP, eng, sem.early) for k, kind, eng in zip((0, 1), "op", halves(on_chip))])
+    direct(chips[2], sem.early)
+    direct(chips[3], sem.late)
+    every = topo.engines(core, T.cores[near])
+    n_wide, n_early, n_late = 4 * len(off_chip), 2 * len(off_chip) + 2 * len(on_chip), 2 * len(off_chip) + 2 * len(every)
+    g.wait_ge(sem.wide, n_wide)
+    send([(near, at(r, HANDED[second][0][0]), at(near, HANDED[second][1]), 4 * CAP, every, sem.late)])
+
+    def copy(dc, ds, a, b, m, done):
+        Y.dma_start(dc[:, a:a + m].bitcast(dt.uint8), T.mc[:, b:b + m].bitcast(dt.uint8)).then_inc(done, 16)
+        Y.dma_start(ds[:, a:a + m], T.ms[:, b:b + m]).then_inc(done, 16)
 
     Y.wait_ge(sem.qa, 1)
-    Y.wait_ge(sem.qb, 1)
-    v = place(r, r)
-    own, prv = CAP * slot_pos(r, r), CAP * slot_pos(r, (r - 1) % N)
-    copy(T.mc, T.ms, RUN * v + (CAP if rising else 0), T.qc, T.qs, own, CAP, sem.selfc)
-    copy(T.mc, T.ms, RUN * v + (0 if rising else CAP), T.qc, T.qs, prv, CAP, sem.selfc)
-    Y.wait_ge(sem.r2, n_wave)
-    draw(64, 6, sem.ca)
-    Y.wait_ge(sem.selfc, 64)
-    Y.wait_ge(sem.rp, n_near)
-    draw(0, 0, sem.ca)
-    Y.wait_ge(sem.r3, n_wave)
-    draw(192, 4, sem.cb)
-    Y.wait_ge(sem.r4, n_wave)
-    draw(128, 2, sem.cb)
+    copy(T.mc, T.ms, at(r, (second, "o")), slots(r), CAP, sem.selfc)
+    Y.wait_ge(sem.wide, n_wide)
+    Y.wait_ge(sem.early, n_early)
+    a = 0
+    for i, run in enumerate(DRAWN[second]):
+        if i == len(DRAWN[second]) - 1:
+            Y.wait_ge(sem.late, n_late)
+        copy(T.wc, T.ws, a, at(r, run[0]), CAP * len(run), sem.drawn)
+        a += CAP * len(run)
 
-    base = r - r % 2
-    mn, pv = slice(0, BW), slice(BW, 2 * BW)
-    V.wait_ge(sem.l_lm, 15 * 16)
+    mn, pv, wo = slice(0, BW), slice(BW, 2 * BW), slice(2 * BW, 3 * BW)
+    V.wait_ge(sem.l_lm, 48)
     V.wait_ge(sem.l_g, 16)
-    V.tensor_scalar(T.k_t[:], T.lm[:], CAP * base, SLOTS, OP.is_lt, OP.mult).then_inc(sem.k1, 1)
-    V.wait_ge(sem.k1, 1)
-    V.tensor_tensor(T.k_b[:], T.lm[:], T.k_t[:], OP.add).then_inc(sem.k2, 1)
+    V.tensor_copy(T.off[0:32, wo], T.lm[0:32, mn]).then_inc(sem.k4, 1)
+    V.tensor_copy(T.k_a[0:32, mn], T.lm[0:32, mn]).then_inc(sem.k1, 1)
+    V.tensor_scalar(T.k_a[0:32, pv], T.lm[0:32, pv], CAP, None, OP.add).then_inc(sem.k1, 1)
+    V.wait_ge(sem.k1, 2)
+    V.tensor_scalar(T.k_b[0:32, :], T.k_a[0:32, :], 7 * RUN, None, OP.bitwise_and).then_inc(sem.k2, 1)
     V.wait_ge(sem.k2, 1)
-    V.tensor_scalar(T.woff[:], T.k_b[:, mn], -CAP * base, None, OP.add).then_inc(sem.k3, 1)
+    V.tensor_tensor(T.k_c[0:32, :], T.k_a[0:32, :], T.k_b[0:32, :], OP.add).then_inc(sem.k3, 1)
     V.wait_ge(sem.k3, 1)
+    V.tensor_scalar(T.off[0:32, mn], T.k_c[0:32, mn], CAP, None, OP.add).then_inc(sem.k4, 1)
+    V.tensor_scalar(T.off[0:32, pv], T.k_c[0:32, pv], -CAP, None, OP.add).then_inc(sem.k4, 1)
+    V.wait_ge(sem.k4, 3)
+    for a in range(1, 4):
+        V.tensor_copy(T.off[32 * a:32 * a + 32, :], T.off[0:32, :]).then_inc(sem.k5, 1)
+    V.wait_ge(sem.k5, 3)
     V.wait_ge(sem.fil, 1)
     V.wait_ge(sem.numd, 1)
-    V.tensor_copy(T.inv[:].indirect(T.woff[:]), T.num[:]).then_inc(sem.invd, 1)
-    V.tensor_scalar(T.k_m[:], T.k_b[:], RUN - 1, None, OP.bitwise_and).then_inc(sem.k4, 1)
-    V.tensor_scalar(T.k_f[:], T.k_b[:, pv], CAP, None, OP.bitwise_and).then_inc(sem.k4, 1)
-    V.tensor_scalar(T.k_d[:], T.k_b[:], 2, -RUN * base, OP.mult, OP.add).then_inc(sem.k4, 1)
-    V.wait_ge(sem.k4, 3)
-    V.tensor_tensor(T.k_e[:], T.k_d[:], T.k_m[:], OP.subtract).then_inc(sem.k5, 1)
-    V.tensor_scalar(T.k_g[:], T.k_f[:], 2, None, OP.mult).then_inc(sem.k5, 1)
-    V.wait_ge(sem.k5, 2)
-    V.tensor_tensor(T.k_p[:], T.k_e[:, pv], T.k_g[:], OP.add).then_inc(sem.k6, 1)
-    V.tensor_scalar(T.coff[:, mn], T.k_e[:, mn], CAP, None, OP.add).then_inc(sem.k7, 1)
-    V.wait_ge(sem.k6, 1)
-    V.tensor_copy(T.coff[:, pv], T.k_p[:]).then_inc(sem.k7, 1)
+    V.tensor_copy(T.inv[:].indirect(T.off[:, wo]), T.num[:]).then_inc(sem.invd, 1)
+    V.wait_ge(sem.invd, 1)
 
-    S.wait_ge(sem.invd, 1)
-    for col, p, a, n in ((0, 0, 256, 64), (1, 0, 0, 64), (1, 64, 192, 64), (2, 0, 64, 128)):
-        S.dma_start(T.idx[p:p + n, col:col + 1], T.inv[0:1, a:a + n]).then_inc(sem.idxd, 16)
+    ia, idd = lay.index(TILE_A[second]), lay.index(TILE_D[second])
+    rows = {"a": lay[ia:ia + 4], "b": sum(DRAWN[second], []), "d": lay[idd + 1:idd + 3]}
+
+    def turn(col, tile, done):
+        for a, (s, _) in enumerate(rows[tile]):
+            s = (base + s) % N
+            V.transpose(T.turned[32 * a:32 * a + 32, CAP * col:CAP * col + CAP],
+                        T.inv[32 * a:32 * a + 32, CAP * s:CAP * s + CAP]).then_inc(done, 1)
+
+    turn(0, "a", sem.t_ab)
+    turn(1, "b", sem.t_ab)
+    V.wait_ge(sem.t_ab, 8)
+    V.tensor_copy(T.idx[:, 0:2], T.turned[:, 0:2 * CAP:CAP]).then_inc(sem.i_ab, 1)
 
     tiles = {
-        "d": (T.mc, T.ms, 8 * RUN, [(6 * RUN, 10 * RUN, 0, S), (0, 2 * RUN, 1, V), (4 * RUN, 6 * RUN, 2, S), (2 * RUN, 4 * RUN, 3, V)]),
-        "a": (T.wc, T.ws, 0, [(0, 5 * RUN, 4, V), (5 * RUN, 10 * RUN, 5, S)]),
-        "b": (T.wc, T.ws, 128, [(0, 5 * RUN, 6, V), (5 * RUN, 10 * RUN, 7, S)]),
+        "a": (T.mc, T.ms, CAP * ia, list(zip(EARLY[second] + LATE[second], (0, 1, 2, 3), (S, S, V, S)))),
+        "d": (T.mc, T.ms, CAP * idd, list(zip(WHOLE[second], (4, 5, 6), (S, V, V)))),
+        "b": (T.wc, T.ws, 0, list(zip(WHOLE[second], (7, 0, 1), (S, V, V)))),
     }
 
     def product(tile, i):
         c, s, a, parts = tiles[tile]
-        lo, hi, bank, _ = parts[i]
+        (first, last), bank, _ = parts[i]
+        lo, hi = at(r, first), at(r, last) + CAP
         P.matmul_mx(T.pp[:, 512 * bank:512 * bank + hi - lo], c[:, a:a + 128], s[:, a:a + 128],
                     T.mc[:, lo:hi], T.ms[:, lo:hi], True, True).then_inc(sem["mm%s%d" % (tile, i)], 1)
 
-    P.wait_ge(sem.r1, n_wave)
-    P.wait_ge(sem.r2, n_wave)
-    product("d", 0)
-    P.wait_ge(sem.selfc, 64)
-    P.wait_ge(sem.rp, n_near)
-    product("d", 1)
-    P.wait_ge(sem.r3, n_wave)
-    product("d", 2)
-    P.wait_ge(sem.r4, n_wave)
-    product("d", 3)
-    for tile, done in (("a", sem.ca), ("b", sem.cb)):
-        P.wait_ge(done, 64)
-        product(tile, 0)
-        product(tile, 1)
-
-    V.wait_ge(sem.k7, 2)
-    S.wait_ge(sem.k7, 2)
-    for tile in "dab":
-        parts = tiles[tile][3]
-        buf, out = T["s_" + tile], T["o_" + tile]
-        for i, (lo, hi, bank, e) in enumerate(parts):
-            e.wait_ge(sem["mm%s%d" % (tile, i)], 1)
-            src = T.pp[:, 512 * bank:512 * bank + hi - lo]
-            done = sem["cp%s%d" % (tile, i)]
-            if e is V:
-                V.tensor_copy(buf[:, lo:hi], src).then_inc(done, 1)
+    def unload(tile, i, done):
+        (first, last), bank, e = tiles[tile][3][i]
+        runs = []
+        for j, (s, kind) in enumerate(lay[lay.index(first):lay.index(last) + 1]):
+            to = RUN * ((base + s) % N) + CAP * ((kind == "o") != (s % 2 == 1))
+            if runs and runs[-1][1] + runs[-1][2] == to:
+                runs[-1][2] += CAP
             else:
-                S.activation(buf[:, lo:hi], src, COPY).then_inc(done, 1)
-        for i in range(len(parts)):
-            V.wait_ge(sem["cp%s%d" % (tile, i)], 1)
-            S.wait_ge(sem["cp%s%d" % (tile, i)], 1)
-        V.tensor_copy(out[:, 0:COLS], buf[:].indirect(T.coff[:, mn])).then_inc(sem["ov" + tile], 1)
-        S.activation(out[:, COLS:2 * COLS], buf[:].indirect(T.coff[:, pv]), COPY).then_inc(sem["os" + tile], 1)
+                runs.append([CAP * j, to, CAP])
+        e.wait_ge(sem["mm%s%d" % (tile, i)], 1)
+        for a, to, m in runs:
+            src, dst = T.pp[:, 512 * bank + a:512 * bank + a + m], T["s_" + tile][:, to:to + m]
+            if e is V:
+                V.tensor_copy(dst, src).then_inc(done, 1)
+            else:
+                S.activation(dst, src, COPY).then_inc(done, 1)
+        return len(runs)
 
-    g.wait_ge(sem.idxd, 64)
-    for col, (tile, lo, n) in enumerate((("d", CAP, 64), ("a", 0, 128), ("b", 0, 128))):
+    def order(tile, waits):
+        for e in (V, S):
+            for s, m in waits:
+                e.wait_ge(s, m)
+        buf, out = T["s_" + tile], T["o_" + tile]
+        V.tensor_copy(out[:, 0:COLS], buf[:].indirect(T.off[:, mn])).then_inc(sem["ov" + tile], 1)
+        S.activation(out[:, COLS:2 * COLS], buf[:].indirect(T.off[:, pv]), COPY).then_inc(sem["os" + tile], 1)
+
+    n_ce = unload("a", 0, sem.c_early) + unload("a", 1, sem.c_early)
+    n_ca = unload("a", 2, sem.c_a) + unload("a", 3, sem.c_a)
+    S.wait_ge(sem.k4, 3)
+    S.wait_ge(sem.k5, 3)
+    order("a", [(sem.c_early, n_ce), (sem.c_a, n_ca)])
+    n_cd = sum(unload("d", i, sem.c_d) for i in range(3))
+    n_cb = sum(unload("b", i, sem.c_b) for i in range(3))
+    order("b", [(sem.c_b, n_cb)])
+    turn(2, "d", sem.t_d)
+    order("d", [(sem.c_d, n_cd)])
+    V.wait_ge(sem.t_d, 2)
+    V.tensor_copy(T.idx[0:64, 2:3], T.turned[0:64, 2 * CAP:2 * CAP + 1]).then_inc(sem.i_d, 1)
+
+    for s, m in ((sem.qa, 1), (sem.qb, 1), (sem.selfc, 32), (sem.wide, n_wide), (sem.early, n_early)):
+        P.wait_ge(s, m)
+    product("a", 0)
+    product("a", 1)
+    P.wait_ge(sem.late, n_late)
+    product("a", 2)
+    product("a", 3)
+    for i in range(3):
+        product("d", i)
+    P.wait_ge(sem.drawn, 32 * len(DRAWN[second]))
+    P.wait_ge(sem.c_early, n_ce)
+    for i in range(3):
+        product("b", i)
+
+    g.wait_ge(sem.i_ab, 1)
+    for col, (tile, lo, m) in enumerate((("a", 0, 128), ("b", 0, 128), ("d", CAP, 64))):
+        if tile == "d":
+            g.wait_ge(sem.i_d, 1)
         g.wait_ge(sem["ov" + tile], 1)
         g.wait_ge(sem["os" + tile], 1)
-        g.indirect_dma_start(T.y[:], IndirectOffsetOnAxis(ap=T.idx[0:n, col:col + 1], axis=0),
-                             T["o_" + tile][lo:lo + n, :], None, bounds_check=COLS - 1, oob_is_err=False).then_inc(sem.stored, 16)
-    g.wait_ge(sem.sent, n_sent)
+        g.indirect_dma_start(T.y[:], IndirectOffsetOnAxis(ap=T.idx[0:m, col:col + 1], axis=0),
+                             T["o_" + tile][lo:lo + m, :], None, bounds_check=COLS - 1, oob_is_err=False).then_inc(sem.stored, 16)
+    g.wait_ge(sem.sent, n_sent[0])
     g.wait_ge(sem.stored, 48)

from concourse.bass import DstId, RemoteDMATransfer, IndirectOffsetOnAxis
from concourse.mybir import dt, AluOpType, ActivationFunctionType

N = 10
COLS = 256
CAP = 32
RUN = 2 * CAP
SLOTS = N * CAP
MOV = N * RUN
LW = 2 * N
BW = COLS // 16
NOROW = 4096.0


def blocks(text):
    return [(int(w[0]), w[1]) for w in text.split()]


SENT = [(k, "q") for k in range(N - 1)]
LAYOUT = [
    SENT + blocks("0p 1p 8p 8o 8j 7j 7o 7p 4p 4o 0o 1o 5o 5p 2p 2o 9o 9p 6p 6o 3o 3p"),
    blocks("2p 2o 3o 3p 8p 8o 7o 7p 4p 4o 1o 0o 9o 9p 9j 6j 6p 6o 5o 5p 0p 1p") + SENT,
]
WIDTH = CAP * len(LAYOUT[0])
TILE_A = [(4, "o"), (4, "o")]
TILE_D = [(6, "p"), (8, "p")]
DRAWN = [[blocks("8o"), blocks("7o"), blocks("2o 9o")], [blocks("6o 5o"), blocks("2o 3o")]]
EARLY = [[blocks("0p 8o"), blocks("7o 5p")], [blocks("4p 9p"), blocks("6p 1p")]]
LATE = [[blocks("2p 9p"), blocks("6p 3p")], [blocks("2p 3p"), blocks("8p 7p")]]
WHOLE = [[blocks("5o 3p"), blocks("0p 8o"), blocks("7o 1o")], [blocks("2p 4o"), blocks("1o 9p"), blocks("6p 1p")]]
HANDED = [(blocks("8o 7o"), (8, "p")), (blocks("9p 6p"), (9, "o"))]

SCRATCH = {
    "snd": ("sbuf", [128, LW], "int32"),
    "soff": ("sbuf", [128, LW], "uint16"),
    "xs": ("sbuf", [128, 4 * COLS], "bfloat16"),
    "h": ("sbuf", [128, 4 * SLOTS], "bfloat16"),
    "mc": ("sbuf", [128, WIDTH], "float8_e4m3fn_x4"),
    "ms": ("sbuf", [128, WIDTH], "uint8"),
    "wc": ("sbuf", [128, 128], "float8_e4m3fn_x4"),
    "ws": ("sbuf", [128, 128], "uint8"),
    "lm": ("sbuf", [128, 2 * BW], "int32"),
    "k_a": ("sbuf", [128, 2 * BW], "int32"),
    "k_b": ("sbuf", [128, 2 * BW], "int32"),
    "k_c": ("sbuf", [128, 2 * BW], "int32"),
    "off": ("sbuf", [128, 3 * BW], "uint16"),
    "nul": ("sbuf", [128, COLS], "float32"),
    "one": ("sbuf", [128, COLS], "float32"),
    "num": ("sbuf", [128, COLS], "float32"),
    "inv": ("sbuf", [128, SLOTS], "float32"),
    "turned": ("sbuf", [128, 3 * CAP], "float32"),
    "idx": ("sbuf", [128, 4], "int32"),
    "pp": ("psum", [128, 512 * 8], "float32"),
}
SEMAPHORES = ["l_send", "l_x", "l_lm", "l_g", "off0", "off1", "gva", "gsa", "gvb", "gsb", "qa", "qb",
              "k1", "k2", "k3", "k4", "k5", "cst", "fil", "numd", "invd", "selfc", "wide", "early", "late",
              "drawn", "t_ab", "t_d", "i_ab", "i_d", "c_early", "sent", "stored"]
for _t in "abd":
    SCRATCH["s_" + _t] = ("sbuf", [128, MOV], "float32")
    SCRATCH["o_" + _t] = ("sbuf", [128, 2 * COLS], "float32")
    SEMAPHORES += ["mm" + _t + str(_p) for _p in range(4 if _t == "a" else 3)] + ["c_" + _t, "ov" + _t, "os" + _t]


def rank_program(g, core, T, topo):
    r = T.rank_of(core)
    if r is None:
        return
    V, S, P, Y, sem = g.vector, g.scalar, g.tensor, g.sync, T.sem
    OP, COPY = AluOpType, ActivationFunctionType.Copy

    def first_of(d):
        return min(k for k in range(N) if topo.chip(T.cores[k]) == topo.chip(T.cores[d]))

    def at(d, block):
        return CAP * LAYOUT[d - first_of(d)].index(block)

    base = first_of(r)
    second = r - base
    near = base + 1 - second
    lay = LAYOUT[second]
    q0 = at(r, (1, "p")) if second else 0

    def slot_pos(d):
        return (r - 1 - d) % N if second else (d - r) % N

    Y.dma_start(T.snd[0:16, :], T.send[:]).then_inc(sem.l_send, 16)
    S.dma_start(T.snd[16:32, :], T.send[:]).then_inc(sem.l_send, 16)
    Y.dma_start(T.xs[:], T.x[:]).then_inc(sem.l_x, 16)
    g.dma_start(T.lm[0:16, 0:BW], T.mine[:]).then_inc(sem.l_g, 16)
    S.dma_start(T.lm[16:32, 0:BW], T.mine[:]).then_inc(sem.l_lm, 16)
    S.dma_start(T.lm[0:16, BW:2 * BW], T.prev[:]).then_inc(sem.l_lm, 16)
    S.dma_start(T.lm[16:32, BW:2 * BW], T.prev[:]).then_inc(sem.l_lm, 16)

    V.memset(T.nul[:], 0.0).then_inc(sem.cst, 1)
    V.memset(T.one[:], 1.0).then_inc(sem.cst, 1)
    V.memset(T.inv[:], NOROW).then_inc(sem.fil, 1)
    V.wait_ge(sem.cst, 2)
    V.tensor_tensor_scan(T.num[:], T.nul[:], T.one[:], -1.0, OP.add, OP.add).then_inc(sem.numd, 1)
    V.wait_ge(sem.l_send, 32)
    n, k = 0, 0
    while k < N:
        slot = (r - 1 - k) % N if second else (r + k) % N
        m = min(N - k, slot + 1 if second else N - slot)
        if second:
            for b in range(2):
                first, stop = 2 * slot + b, 2 * (slot - m + 1) + b - 1
                src = T.snd[0:32, first::-2] if stop < 0 else T.snd[0:32, first:stop:-2]
                V.tensor_scalar(T.soff[0:32, 2 * k + b:2 * (k + m):2], src, 4, 0, OP.mult, OP.max).then_inc(sem.off0, 1)
                n += 1
        else:
            V.tensor_scalar(T.soff[0:32, 2 * k:2 * (k + m)], T.snd[0:32, 2 * slot:2 * (slot + m)], 4, 0, OP.mult, OP.max).then_inc(sem.off0, 1)
            n += 1
        k += m
    V.wait_ge(sem.off0, n)
    for a in range(1, 4):
        V.tensor_copy(T.soff[32 * a:32 * a + 32, :], T.soff[0:32, :]).then_inc(sem.off1, 1)

    stage = [(6, 10), (0, 6)] if second else [(0, 4), (4, 10)]
    gv, gs, qd = [sem.gva, sem.gvb], [sem.gsa, sem.gsb], [sem.qa, sem.qb]
    for e in (V, S):
        e.wait_ge(sem.off0, n)
        e.wait_ge(sem.off1, 3)
        e.wait_ge(sem.l_x, 16)
    for w in range(2):
        lo, hi = stage[w]
        for t in range(4):
            out = T.h[:, 128 * lo + t:128 * hi:4]
            src = T.xs[:, t:4 * COLS].indirect(T.soff[:, 2 * lo:2 * hi])
            if t < 2:
                V.tensor_copy(out, src).then_inc(gv[w], 1)
            else:
                S.activation(out, src, COPY).then_inc(gs[w], 1)
        V.wait_ge(gv[w], 2)
        V.wait_ge(gs[w], 2)
        a, b = q0 + CAP * lo, q0 + CAP * hi
        V.quantize_mx(T.mc[:, a:b], T.ms[:, a:b], T.h[:, 128 * lo:128 * hi]).then_inc(qd[w], 1)

    n_sent = [0]

    def send(moves):
        for codes, buf in ((True, T.mc), (False, T.ms)):
            calls = []
            for d, a, b, m, eng, done in moves:
                rid, pid, _ = topo.addr(T.cores[d])
                src, dst = buf[:, a:a + m], buf[:, b:b + m]
                if codes:
                    src, dst = src.bitcast(dt.uint8), dst.bitcast(dt.uint8)
                calls.append(RemoteDMATransfer(dst_ids=[DstId(rid=rid, pnc=pid)], dma_engine_mask=sum(1 << e for e in eng),
                                               remote_sem=done, src=src, dst=dst))
                n_sent[0] += len(eng)
            g.remote_dma_fused(calls, local_sem=sem.sent)

    def halves(e):
        return e[:len(e) // 2], e[len(e) // 2:]

    def kept(d, kinds):
        return min(at(d, ((r - first_of(d)) % N, k)) for k in kinds)

    def slots(*ranks):
        return q0 + CAP * min(slot_pos(d % N) for d in ranks)

    chips = [(base + 2 * k) % N for k in range(1, N // 2)]
    off_chip = topo.engines(core, T.cores[chips[0]])
    on_chip = [e for e in topo.engines(core, T.cores[near]) if e not in off_chip]
    for w in range(2):
        c = chips[w]
        d = c + (second if w == 0 else 1 - second)
        g.wait_ge(qd[w], 1)
        send([(d, slots(c - 1, c, c + 1), kept(d, "opj"), 3 * CAP, topo.engines(core, T.cores[d]), sem.wide)])
    def direct(c, done):
        send([(d, slots(d - 1, d), kept(d, "op"), RUN, halves(topo.engines(core, T.cores[d]))[d - c], done) for d in (c, c + 1)])

    send([(near, slots(near - k), kept(near, kind), CAP, eng, sem.early) for k, kind, eng in zip((0, 1), "op", halves(on_chip))])
    direct(chips[2], sem.early)
    direct(chips[3], sem.late)
    every = topo.engines(core, T.cores[near])
    n_wide, n_early, n_late = 4 * len(off_chip), 2 * len(off_chip) + 2 * len(on_chip), 2 * len(off_chip) + 2 * len(every)
    g.wait_ge(sem.wide, n_wide)
    send([(near, at(r, HANDED[second][0][0]), at(near, HANDED[second][1]), 4 * CAP, every, sem.late)])

    def copy(dc, ds, a, b, m, done):
        Y.dma_start(dc[:, a:a + m].bitcast(dt.uint8), T.mc[:, b:b + m].bitcast(dt.uint8)).then_inc(done, 16)
        Y.dma_start(ds[:, a:a + m], T.ms[:, b:b + m]).then_inc(done, 16)

    Y.wait_ge(sem.qa, 1)
    copy(T.mc, T.ms, at(r, (second, "o")), slots(r), CAP, sem.selfc)
    Y.wait_ge(sem.wide, n_wide)
    Y.wait_ge(sem.early, n_early)
    a = 0
    for i, run in enumerate(DRAWN[second]):
        if i == len(DRAWN[second]) - 1:
            Y.wait_ge(sem.late, n_late)
        copy(T.wc, T.ws, a, at(r, run[0]), CAP * len(run), sem.drawn)
        a += CAP * len(run)

    mn, pv, wo = slice(0, BW), slice(BW, 2 * BW), slice(2 * BW, 3 * BW)
    V.wait_ge(sem.l_lm, 48)
    V.wait_ge(sem.l_g, 16)
    V.tensor_copy(T.off[0:32, wo], T.lm[0:32, mn]).then_inc(sem.k4, 1)
    V.tensor_copy(T.k_a[0:32, mn], T.lm[0:32, mn]).then_inc(sem.k1, 1)
    V.tensor_scalar(T.k_a[0:32, pv], T.lm[0:32, pv], CAP, None, OP.add).then_inc(sem.k1, 1)
    V.wait_ge(sem.k1, 2)
    V.tensor_scalar(T.k_b[0:32, :], T.k_a[0:32, :], 7 * RUN, None, OP.bitwise_and).then_inc(sem.k2, 1)
    V.wait_ge(sem.k2, 1)
    V.tensor_tensor(T.k_c[0:32, :], T.k_a[0:32, :], T.k_b[0:32, :], OP.add).then_inc(sem.k3, 1)
    V.wait_ge(sem.k3, 1)
    V.tensor_scalar(T.off[0:32, mn], T.k_c[0:32, mn], CAP, None, OP.add).then_inc(sem.k4, 1)
    V.tensor_scalar(T.off[0:32, pv], T.k_c[0:32, pv], -CAP, None, OP.add).then_inc(sem.k4, 1)
    V.wait_ge(sem.k4, 3)
    for a in range(1, 4):
        V.tensor_copy(T.off[32 * a:32 * a + 32, :], T.off[0:32, :]).then_inc(sem.k5, 1)
    V.wait_ge(sem.k5, 3)
    V.wait_ge(sem.fil, 1)
    V.wait_ge(sem.numd, 1)
    V.tensor_copy(T.inv[:].indirect(T.off[:, wo]), T.num[:]).then_inc(sem.invd, 1)
    V.wait_ge(sem.invd, 1)

    ia, idd = lay.index(TILE_A[second]), lay.index(TILE_D[second])
    rows = {"a": lay[ia:ia + 4], "b": sum(DRAWN[second], []), "d": lay[idd + 1:idd + 3]}

    def turn(col, tile, done):
        for a, (s, _) in enumerate(rows[tile]):
            s = (base + s) % N
            V.transpose(T.turned[32 * a:32 * a + 32, CAP * col:CAP * col + CAP],
                        T.inv[32 * a:32 * a + 32, CAP * s:CAP * s + CAP]).then_inc(done, 1)

    turn(0, "a", sem.t_ab)
    turn(1, "b", sem.t_ab)
    V.wait_ge(sem.t_ab, 8)
    V.tensor_copy(T.idx[:, 0:2], T.turned[:, 0:2 * CAP:CAP]).then_inc(sem.i_ab, 1)

    tiles = {
        "a": (T.mc, T.ms, CAP * ia, list(zip(EARLY[second] + LATE[second], (0, 1, 2, 3), (S, S, V, S)))),
        "d": (T.mc, T.ms, CAP * idd, list(zip(WHOLE[second], (4, 5, 6), (S, V, V)))),
        "b": (T.wc, T.ws, 0, list(zip(WHOLE[second], (7, 0, 1), (S, V, V)))),
    }

    def product(tile, i):
        c, s, a, parts = tiles[tile]
        (first, last), bank, _ = parts[i]
        lo, hi = at(r, first), at(r, last) + CAP
        P.matmul_mx(T.pp[:, 512 * bank:512 * bank + hi - lo], c[:, a:a + 128], s[:, a:a + 128],
                    T.mc[:, lo:hi], T.ms[:, lo:hi], True, True).then_inc(sem["mm%s%d" % (tile, i)], 1)

    def unload(tile, i, done):
        (first, last), bank, e = tiles[tile][3][i]
        runs = []
        for j, (s, kind) in enumerate(lay[lay.index(first):lay.index(last) + 1]):
            to = RUN * ((base + s) % N) + CAP * ((kind == "o") != (s % 2 == 1))
            if runs and runs[-1][1] + runs[-1][2] == to:
                runs[-1][2] += CAP
            else:
                runs.append([CAP * j, to, CAP])
        e.wait_ge(sem["mm%s%d" % (tile, i)], 1)
        for a, to, m in runs:
            src, dst = T.pp[:, 512 * bank + a:512 * bank + a + m], T["s_" + tile][:, to:to + m]
            if e is V:
                V.tensor_copy(dst, src).then_inc(done, 1)
            else:
                S.activation(dst, src, COPY).then_inc(done, 1)
        return len(runs)

    def order(tile, waits):
        for e in (V, S):
            for s, m in waits:
                e.wait_ge(s, m)
        buf, out = T["s_" + tile], T["o_" + tile]
        V.tensor_copy(out[:, 0:COLS], buf[:].indirect(T.off[:, mn])).then_inc(sem["ov" + tile], 1)
        S.activation(out[:, COLS:2 * COLS], buf[:].indirect(T.off[:, pv]), COPY).then_inc(sem["os" + tile], 1)

    n_ce = unload("a", 0, sem.c_early) + unload("a", 1, sem.c_early)
    n_ca = unload("a", 2, sem.c_a) + unload("a", 3, sem.c_a)
    S.wait_ge(sem.k4, 3)
    S.wait_ge(sem.k5, 3)
    order("a", [(sem.c_early, n_ce), (sem.c_a, n_ca)])
    n_cd = sum(unload("d", i, sem.c_d) for i in range(3))
    n_cb = sum(unload("b", i, sem.c_b) for i in range(3))
    order("b", [(sem.c_b, n_cb)])
    turn(2, "d", sem.t_d)
    order("d", [(sem.c_d, n_cd)])
    V.wait_ge(sem.t_d, 2)
    V.tensor_copy(T.idx[0:64, 2:3], T.turned[0:64, 2 * CAP:2 * CAP + 1]).then_inc(sem.i_d, 1)

    for s, m in ((sem.qa, 1), (sem.qb, 1), (sem.selfc, 32), (sem.wide, n_wide), (sem.early, n_early)):
        P.wait_ge(s, m)
    product("a", 0)
    product("a", 1)
    P.wait_ge(sem.late, n_late)
    product("a", 2)
    product("a", 3)
    for i in range(3):
        product("d", i)
    P.wait_ge(sem.drawn, 32 * len(DRAWN[second]))
    P.wait_ge(sem.c_early, n_ce)
    for i in range(3):
        product("b", i)

    g.wait_ge(sem.i_ab, 1)
    for col, (tile, lo, m) in enumerate((("a", 0, 128), ("b", 0, 128), ("d", CAP, 64))):
        if tile == "d":
            g.wait_ge(sem.i_d, 1)
        g.wait_ge(sem["ov" + tile], 1)
        g.wait_ge(sem["os" + tile], 1)
        g.indirect_dma_start(T.y[:], IndirectOffsetOnAxis(ap=T.idx[0:m, col:col + 1], axis=0),
                             T["o_" + tile][lo:lo + m, :], None, bounds_check=COLS - 1, oob_is_err=False).then_inc(sem.stored, 16)
    g.wait_ge(sem.sent, n_sent[0])
    g.wait_ge(sem.stored, 48)
